import numpy as np
import ml_dtypes


def mxq(x, axis, fmt="e4m3"):
    dtype, down = {"e4m3": (ml_dtypes.float8_e4m3fn, 7), "e5m2": (ml_dtypes.float8_e5m2, 14)}[fmt]
    v = np.moveaxis(np.asarray(x, np.float32).astype(ml_dtypes.bfloat16).astype(np.float64), axis, -1)
    blocks = v.reshape(v.shape[:-1] + (-1, 32))
    amax = np.abs(blocks).max(-1, keepdims=True)
    byte = np.maximum(np.where(amax > 0, np.frexp(amax)[1] - 1 + 127, 0) - down, 1)
    scale = np.exp2(byte - 127.0)
    codes = (blocks / scale).astype(np.float32).astype(dtype).astype(np.float64)
    return np.moveaxis((codes * scale).reshape(v.shape), -1, axis)


WIDE = False


def mx_kscale(k):
    if not WIDE:
        return np.ones(k)
    levels = np.array([10, -10, 5, -5, 0])
    if k % 512:
        return np.exp2(np.random.permutation(np.resize(levels, k // 32))).repeat(32)
    a = np.empty((k // 512, 16))
    for p in range(k // 512):
        a[p, :8] = np.random.permutation(np.resize(levels, 8))
        for g in range(8):
            far = levels[np.abs(levels - a[p, g]) >= 10]
            a[p, g + 8] = far[np.random.randint(len(far))]
    return np.exp2(a.ravel()).repeat(32)


def f64(x):
    return np.asarray(x).astype(np.float64)


def striped8(idx):
    return np.asarray(idx).reshape(8, -1, 16).transpose(0, 2, 1).reshape(128, -1).astype(np.uint16)


def unstriped8(offs):
    return offs.reshape(8, 16, -1).transpose(0, 2, 1).reshape(8, -1).astype(np.int64)


def pick8(x, idx, run):
    r = np.arange(len(x))
    return x[r[:, None], idx[r % (8 * run) // run]]


E2M1 = np.array([0.0, 0.5, 1.0, 1.5, 2.0, 3.0, 4.0, 6.0, -0.0, -0.5, -1.0, -1.5, -2.0, -3.0, -4.0, -6.0])


def pack_weight(w, fmt):
    k, n = w.shape
    w = f64(np.asarray(w, np.float32).astype(ml_dtypes.bfloat16)).reshape(k // 32, 32, n)
    amax = np.abs(w).max(1)
    if fmt == "e4m3":
        byte = np.frexp(amax)[1] - 1 + 127 - 7
    else:
        mant, ex = np.frexp(amax / 6.0)
        byte = np.where(mant > 0.5, ex, ex - 1) + 127
    byte = np.clip(np.where(amax > 0, byte, 1), 1, 254)
    scaled = (w * np.exp2(127.0 - byte)[:, None, :]).reshape(k, n).astype(np.float32)
    by_word = np.ascontiguousarray(scaled.reshape(k // 512, 128, 4, n).transpose(0, 1, 3, 2))
    if fmt == "e4m3":
        words = by_word.astype(ml_dtypes.float8_e4m3fn).view(np.uint8)
    else:
        c = by_word.astype(ml_dtypes.float4_e2m1fn).view(np.uint8) & 0xF
        words = (c[..., 0::2] | (c[..., 1::2] << 4)).reshape(k // 512, 128, 2 * n)
    return np.ascontiguousarray(words), np.ascontiguousarray(byte.astype(np.uint8).reshape(k // 512, 16, n))


def unpack_weight(words, scales, fmt):
    g, _, n = scales.shape
    words = np.ascontiguousarray(words).reshape(g, 128, n, -1)
    if fmt == "e4m3":
        vals = words.view(ml_dtypes.float8_e4m3fn).astype(np.float64)
    else:
        nib = np.empty((g, 128, n, 4), np.uint8)
        nib[..., 0::2] = words & 0xF
        nib[..., 1::2] = words >> 4
        vals = E2M1[nib]
    vals = vals * np.repeat(np.exp2(scales.astype(np.float64) - 127.0), 8, axis=1)[..., None]
    return vals.transpose(0, 1, 3, 2).reshape(g * 512, n)


D, V, Q, I = 512, 2048, 128, 512


def setup_inputs():
    n = np.random.standard_normal
    idx = np.stack([np.random.permutation(V)[:I] for _ in range(8)])
    fd = mx_kscale(D)
    vocp = pack_weight(n((D, V)) / fd[:, None], "e4m3")
    return {
        "hid": (n((D, Q)) * 1.0 / np.sqrt(D) * fd[:, None]).astype(np.float32),
        "voc_words": vocp[0],
        "voc_scales": vocp[1],
        "aim": (np.random.uniform(4.0, 5.5, (Q, 1))).astype(np.float32),
        "old": (0.5 * n((Q, V))).astype(np.float32),
        "offs": striped8(idx),
    }


def reference(hid, voc_words, voc_scales, aim, old, offs):
    idx = unstriped8(offs)
    vocu = unpack_weight(voc_words, voc_scales, "e4m3")
    hidq = mxq(f64(hid), 0, "e4m3")
    a = hidq.T @ vocu
    m1 = np.max(a, axis=1, keepdims=True)
    lx = pick8(a, idx, 16) - m1
    px = np.exp(lx)
    zl = np.sum(px, axis=1, keepdims=True)
    et = np.log(zl) - np.sum(px * lx, axis=1, keepdims=True) / zl
    det = (et - f64(aim)) * 2.0
    dzl = det / zl - det * (-1.0) * np.sum(px * lx, axis=1, keepdims=True) / np.square(zl)
    dpx = det * (-1.0) / zl * lx + dzl
    dlx = det * (-1.0) / zl * px + dpx * px
    s1 = np.zeros((Q, V))
    s1[np.arange(Q)[:, None], idx[np.arange(Q) % 128 // 16]] = dlx
    y = s1 * 256.0 + f64(old)
    return y

@@ -1,0 +1,147 @@
+from contextlib import ExitStack
+
+import concourse.mybir as mybir
+
+D, V, Q, I = 512, 2048, 128, 512
+FLOPS = 2 * D * V * Q
+
+F32 = mybir.dt.float32
+BF16 = mybir.dt.bfloat16
+I32 = mybir.dt.int32
+U32 = mybir.dt.uint32
+U16 = mybir.dt.uint16
+U8 = mybir.dt.uint8
+FP8X4 = mybir.dt.float8_e4m3fn_x4
+ALU = mybir.AluOpType
+ACT = mybir.ActivationFunctionType
+AX = mybir.AxisListType
+
+P = 128
+PACK = 4
+PLANE = 512
+MM = 256
+WORD_LOADS = (768, 768, 512)
+SCORE_RUNS = (256, 512, 512, 512, 256)
+OUT_RUNS = (256, 512, 512, 512, 256)
+
+
+def runs(widths):
+    first = 0
+    out = []
+    for w in widths:
+        out.append((first, first + w))
+        first = first + w
+    return out
+
+
+def tile_attend_blistspread_heads_kernel(tc, hid, voc_words, voc_scales, aim, old, offs, out):
+    nc = tc.nc
+    with ExitStack() as ctx:
+        pool = ctx.enter_context(tc.tile_pool(name="pool", bufs=1))
+        psum = ctx.enter_context(tc.psum_pool(name="psum", bufs=1))
+
+        offsets = pool.tile([P, I // 16], U16, name="offsets")
+        voc_plane = pool.tile([P, PLANE], U8, name="voc_plane", align_bytes=64)
+        nc.vector.memset(voc_plane[:].bitcast(I32), 0)
+        warm_in = pool.tile([P, 1], F32, name="warm_in")
+        nc.vector.memset(warm_in[:], 0.0)
+        spread = pool.tile([P, V], F32, name="spread")
+        nc.vector.memset(spread[:], 0.0)
+
+        hid_raw = pool.tile([P, PACK, Q], F32, name="hid_raw")
+        nc.sync.dma_start(out=hid_raw[:], in_=hid.rearrange("(p t) q -> p t q", t=PACK))
+        for quad in range(4):
+            rows = voc_scales[0, 4 * quad : 4 * quad + 4, :].bitcast(I32)
+            nc.sync.dma_start(
+                out=voc_plane[32 * quad : 32 * quad + 16, :].bitcast(I32),
+                in_=rows.rearrange("r (j c) -> j r c", j=V // PLANE),
+            )
+        words_hbm = voc_words[0].rearrange("p n t -> p (n t)").bitcast(I32)
+        word_tiles = []
+        for n, (lo, hi) in enumerate(runs(WORD_LOADS)):
+            words = pool.tile([P, hi - lo], U32, name="words%d" % n, align_bytes=64)
+            nc.sync.dma_start(out=words[:].bitcast(I32), in_=words_hbm[:, lo:hi])
+            word_tiles.append((lo, hi, words))
+        nc.sync.dma_start(offsets[:], offs)
+        aim_col = pool.tile([P, 1], F32, name="aim_col")
+        nc.sync.dma_start(out=aim_col[:], in_=aim)
+        old_sb = pool.tile([P, V], F32, name="old_sb")
+        nc.sync.dma_start(out=old_sb[:], in_=old)
+
+        warm_out = pool.tile([P, 1], F32, name="warm_out")
+        nc.scalar.activation(warm_out[:], warm_in[:], ACT.Exp)
+
+        hid_bf = pool.tile([P, Q, PACK], BF16, name="hid_bf", align_bytes=64)
+        nc.vector.tensor_copy(
+            out=hid_bf[:].rearrange("p (c i) t -> p c t i", i=4),
+            in_=hid_raw[:].rearrange("p t (c i) -> p c t i", i=4),
+        )
+        hid_codes = pool.tile([P, Q], U32, name="hid_codes", align_bytes=64)
+        hid_plane = pool.tile([P, Q], U8, name="hid_plane", align_bytes=64)
+        nc.vector.quantize_mx(
+            out=hid_codes[:].bitcast(FP8X4),
+            scales=hid_plane[:],
+            in_=hid_bf[:].rearrange("p q t -> p (q t)"),
+        )
+
+        scores = pool.tile([P, V], F32, name="scores")
+        run_max = pool.tile([P, len(SCORE_RUNS)], F32, name="run_max")
+        for n, (lo, hi) in enumerate(runs(SCORE_RUNS)):
+            bank = psum.tile([P, 512], F32, name="bank%d" % n)
+            for first in range(lo, hi, MM):
+                w_lo, w_hi, words = [w for w in word_tiles if w[0] <= first < w[1]][0]
+                j, c = divmod(first, PLANE)
+                nc.tensor.matmul_mx(
+                    out=bank[:, first - lo : first - lo + MM],
+                    lhsT=hid_codes[:].bitcast(FP8X4),
+                    lhsT_scale=hid_plane[:],
+                    rhs=words[:, first - w_lo : first - w_lo + MM].bitcast(FP8X4),
+                    rhs_scale=voc_plane[4 * j : P, c : c + MM],
+                    start=True,
+                    stop=True,
+                )
+            nc.vector.tensor_scalar(
+                out=scores[:, lo:hi], in0=bank[:, 0 : hi - lo], scalar1=1.0, scalar2=None,
+                op0=ALU.mult, op1=ALU.max, accum_out=run_max[:, n : n + 1],
+            )
+        neg_max = pool.tile([P, 1], F32, name="neg_max")
+        nc.vector.tensor_reduce(neg_max[:], run_max[:], AX.X, ALU.max, negate=True)
+        picked = pool.tile([P, I], F32, name="picked")
+        nc.vector.tensor_copy(picked[:], scores[:].indirect(offsets[:]))
+        px = pool.tile([P, I], F32, name="px")
+        z = pool.tile([P, 1], F32, name="z")
+        nc.scalar.activation(px[:], picked[:], ACT.Exp, bias=neg_max[:], accum_out=z[:])
+        lx = pool.tile([P, I], F32, name="lx")
+        nc.vector.tensor_scalar(out=lx[:], in0=picked[:], scalar1=neg_max[:], scalar2=None, op0=ALU.add)
+        px_lx = pool.tile([P, I], F32, name="px_lx")
+        s = pool.tile([P, 1], F32, name="s")
+        nc.vector.scalar_tensor_tensor(
+            out=px_lx[:], in0=lx[:], scalar=1.0, in1=px[:], op0=ALU.mult, op1=ALU.mult, accum_out=s[:]
+        )
+        rz = pool.tile([P, 1], F32, name="rz")
+        nc.vector.reciprocal(rz[:], z[:])
+        dev = pool.tile([P, I], F32, name="dev")
+        nc.vector.tensor_scalar(
+            out=dev[:], in0=lx[:], scalar1=z[:], scalar2=s[:], op0=ALU.mult, op1=ALU.subtract
+        )
+        nc.vector.tensor_tensor(spread[:].indirect(offsets[:]), px[:], dev[:], ALU.mult)
+
+        ln_z = pool.tile([P, 1], F32, name="ln_z")
+        nc.scalar.activation(ln_z[:], z[:], ACT.Ln)
+        mean_aim = pool.tile([P, 1], F32, name="mean_aim")
+        nc.scalar.activation(mean_aim[:], s[:], ACT.Identity, bias=aim_col[:], scale=rz[:])
+        miss = pool.tile([P, 1], F32, name="miss")
+        nc.scalar.activation(miss[:], ln_z[:], ACT.Identity, bias=mean_aim[:], scale=-1.0)
+        miss_z = pool.tile([P, 1], F32, name="miss_z")
+        nc.scalar.activation(miss_z[:], miss[:], ACT.Copy, scale=rz[:])
+        rz512 = pool.tile([P, 1], F32, name="rz512")
+        nc.scalar.activation(rz512[:], rz[:], ACT.Copy, scale=512.0)
+        factor = pool.tile([P, 1], F32, name="factor")
+        nc.scalar.activation(factor[:], miss_z[:], ACT.Copy, scale=rz512[:])
+
+        for n, (lo, hi) in enumerate(runs(OUT_RUNS)):
+            result = pool.tile([P, hi - lo], F32, name="result%d" % n)
+            nc.vector.scalar_tensor_tensor(
+                out=result[:], in0=spread[:, lo:hi], scalar=factor[:], in1=old_sb[:, lo:hi], op0=ALU.mult, op1=ALU.add
+            )
+            nc.sync.dma_start(out=out[:, lo:hi], in_=result[:])

@@ -20,8 +20,8 @@ P = 128
 PACK = 4
 PLANE = 512
 MM = 256
-WORD_LOADS = (768, 768, 512)
-SCORE_RUNS = (256, 512, 512, 512, 256)
+WORD_LOADS = (512, 768, 768)
+SCORE_RUNS = (256, 256, 512, 512, 512)
 OUT_RUNS = (256, 512, 512, 512, 256)
 
 
@@ -46,22 +46,23 @@ def tile_attend_blistspread_heads_kernel(tc, hid, voc_words, voc_scales, aim, ol
         warm_in = pool.tile([P, 1], F32, name="warm_in")
         nc.vector.memset(warm_in[:], 0.0)
         spread = pool.tile([P, V], F32, name="spread")
-        nc.vector.memset(spread[:], 0.0)
+        nc.vector.memset(spread[:].bitcast(I32), 0)
 
         hid_raw = pool.tile([P, PACK, Q], F32, name="hid_raw")
         nc.sync.dma_start(out=hid_raw[:], in_=hid.rearrange("(p t) q -> p t q", t=PACK))
-        for quad in range(4):
-            rows = voc_scales[0, 4 * quad : 4 * quad + 4, :].bitcast(I32)
-            nc.sync.dma_start(
-                out=voc_plane[32 * quad : 32 * quad + 16, :].bitcast(I32),
-                in_=rows.rearrange("r (j c) -> j r c", j=V // PLANE),
-            )
         words_hbm = voc_words[0].rearrange("p n t -> p (n t)").bitcast(I32)
         word_tiles = []
         for n, (lo, hi) in enumerate(runs(WORD_LOADS)):
             words = pool.tile([P, hi - lo], U32, name="words%d" % n, align_bytes=64)
             nc.sync.dma_start(out=words[:].bitcast(I32), in_=words_hbm[:, lo:hi])
             word_tiles.append((lo, hi, words))
+            if n == 0:
+                for quad in range(4):
+                    rows = voc_scales[0, 4 * quad : 4 * quad + 4, :].bitcast(I32)
+                    nc.sync.dma_start(
+                        out=voc_plane[32 * quad : 32 * quad + 16, :].bitcast(I32),
+                        in_=rows.rearrange("r (j c) -> j r c", j=V // PLANE),
+                    )
         nc.sync.dma_start(offsets[:], offs)
         aim_col = pool.tile([P, 1], F32, name="aim_col")
         nc.sync.dma_start(out=aim_col[:], in_=aim)
@@ -73,8 +74,12 @@ def tile_attend_blistspread_heads_kernel(tc, hid, voc_words, voc_scales, aim, ol
 
         hid_bf = pool.tile([P, Q, PACK], BF16, name="hid_bf", align_bytes=64)
         nc.vector.tensor_copy(
-            out=hid_bf[:].rearrange("p (c i) t -> p c t i", i=4),
-            in_=hid_raw[:].rearrange("p t (c i) -> p c t i", i=4),
+            out=hid_bf[:, 0:88, :].rearrange("p (c i) t -> p c t i", i=4),
+            in_=hid_raw[:, :, 0:88].rearrange("p t (c i) -> p c t i", i=4),
+        )
+        nc.scalar.copy(
+            out=hid_bf[:, 88:Q, :].rearrange("p (c i) t -> p c t i", i=4),
+            in_=hid_raw[:, :, 88:Q].rearrange("p t (c i) -> p c t i", i=4),
         )
         hid_codes = pool.tile([P, Q], U32, name="hid_codes", align_bytes=64)
         hid_plane = pool.tile([P, Q], U8, name="hid_plane", align_bytes=64)
@@ -116,7 +121,7 @@ def tile_attend_blistspread_heads_kernel(tc, hid, voc_words, voc_scales, aim, ol
         px_lx = pool.tile([P, I], F32, name="px_lx")
         s = pool.tile([P, 1], F32, name="s")
         nc.vector.scalar_tensor_tensor(
-            out=px_lx[:], in0=lx[:], scalar=1.0, in1=px[:], op0=ALU.mult, op1=ALU.mult, accum_out=s[:]
+            out=px_lx[:], in0=picked[:], scalar=neg_max[:], in1=px[:], op0=ALU.add, op1=ALU.mult, accum_out=s[:]
         )
         rz = pool.tile([P, 1], F32, name="rz")
         nc.vector.reciprocal(rz[:], z[:])

@@ -20,7 +20,7 @@ P = 128
 PACK = 4
 PLANE = 512
 MM = 256
-WORD_LOADS = (512, 768, 768)
+WORD_LOADS = (512, 512, 512, 512)
 SCORE_RUNS = (256, 256, 512, 512, 512)
 OUT_RUNS = (256, 512, 512, 512, 256)
 

from contextlib import ExitStack

import concourse.mybir as mybir

D, V, Q, I = 512, 2048, 128, 512
FLOPS = 2 * D * V * Q

F32 = mybir.dt.float32
BF16 = mybir.dt.bfloat16
I32 = mybir.dt.int32
U32 = mybir.dt.uint32
U16 = mybir.dt.uint16
U8 = mybir.dt.uint8
FP8X4 = mybir.dt.float8_e4m3fn_x4
ALU = mybir.AluOpType
ACT = mybir.ActivationFunctionType
AX = mybir.AxisListType

P = 128
PACK = 4
PLANE = 512
MM = 256
WORD_LOADS = (512, 512, 512, 512)
SCORE_RUNS = (256, 256, 512, 512, 512)
OUT_RUNS = (256, 512, 512, 512, 256)


def runs(widths):
    first = 0
    out = []
    for w in widths:
        out.append((first, first + w))
        first = first + w
    return out


def tile_attend_blistspread_heads_kernel(tc, hid, voc_words, voc_scales, aim, old, offs, out):
    nc = tc.nc
    with ExitStack() as ctx:
        pool = ctx.enter_context(tc.tile_pool(name="pool", bufs=1))
        psum = ctx.enter_context(tc.psum_pool(name="psum", bufs=1))

        offsets = pool.tile([P, I // 16], U16, name="offsets")
        voc_plane = pool.tile([P, PLANE], U8, name="voc_plane", align_bytes=64)
        nc.vector.memset(voc_plane[:].bitcast(I32), 0)
        warm_in = pool.tile([P, 1], F32, name="warm_in")
        nc.vector.memset(warm_in[:], 0.0)
        spread = pool.tile([P, V], F32, name="spread")
        nc.vector.memset(spread[:].bitcast(I32), 0)

        hid_raw = pool.tile([P, PACK, Q], F32, name="hid_raw")
        nc.sync.dma_start(out=hid_raw[:], in_=hid.rearrange("(p t) q -> p t q", t=PACK))
        words_hbm = voc_words[0].rearrange("p n t -> p (n t)").bitcast(I32)
        word_tiles = []
        for n, (lo, hi) in enumerate(runs(WORD_LOADS)):
            words = pool.tile([P, hi - lo], U32, name="words%d" % n, align_bytes=64)
            nc.sync.dma_start(out=words[:].bitcast(I32), in_=words_hbm[:, lo:hi])
            word_tiles.append((lo, hi, words))
            if n == 0:
                for quad in range(4):
                    rows = voc_scales[0, 4 * quad : 4 * quad + 4, :].bitcast(I32)
                    nc.sync.dma_start(
                        out=voc_plane[32 * quad : 32 * quad + 16, :].bitcast(I32),
                        in_=rows.rearrange("r (j c) -> j r c", j=V // PLANE),
                    )
        nc.sync.dma_start(offsets[:], offs)
        aim_col = pool.tile([P, 1], F32, name="aim_col")
        nc.sync.dma_start(out=aim_col[:], in_=aim)
        old_sb = pool.tile([P, V], F32, name="old_sb")
        nc.sync.dma_start(out=old_sb[:], in_=old)

        warm_out = pool.tile([P, 1], F32, name="warm_out")
        nc.scalar.activation(warm_out[:], warm_in[:], ACT.Exp)

        hid_bf = pool.tile([P, Q, PACK], BF16, name="hid_bf", align_bytes=64)
        nc.vector.tensor_copy(
            out=hid_bf[:, 0:88, :].rearrange("p (c i) t -> p c t i", i=4),
            in_=hid_raw[:, :, 0:88].rearrange("p t (c i) -> p c t i", i=4),
        )
        nc.scalar.copy(
            out=hid_bf[:, 88:Q, :].rearrange("p (c i) t -> p c t i", i=4),
            in_=hid_raw[:, :, 88:Q].rearrange("p t (c i) -> p c t i", i=4),
        )
        hid_codes = pool.tile([P, Q], U32, name="hid_codes", align_bytes=64)
        hid_plane = pool.tile([P, Q], U8, name="hid_plane", align_bytes=64)
        nc.vector.quantize_mx(
            out=hid_codes[:].bitcast(FP8X4),
            scales=hid_plane[:],
            in_=hid_bf[:].rearrange("p q t -> p (q t)"),
        )

        scores = pool.tile([P, V], F32, name="scores")
        run_max = pool.tile([P, len(SCORE_RUNS)], F32, name="run_max")
        for n, (lo, hi) in enumerate(runs(SCORE_RUNS)):
            bank = psum.tile([P, 512], F32, name="bank%d" % n)
            for first in range(lo, hi, MM):
                w_lo, w_hi, words = [w for w in word_tiles if w[0] <= first < w[1]][0]
                j, c = divmod(first, PLANE)
                nc.tensor.matmul_mx(
                    out=bank[:, first - lo : first - lo + MM],
                    lhsT=hid_codes[:].bitcast(FP8X4),
                    lhsT_scale=hid_plane[:],
                    rhs=words[:, first - w_lo : first - w_lo + MM].bitcast(FP8X4),
                    rhs_scale=voc_plane[4 * j : P, c : c + MM],
                    start=True,
                    stop=True,
                )
            nc.vector.tensor_scalar(
                out=scores[:, lo:hi], in0=bank[:, 0 : hi - lo], scalar1=1.0, scalar2=None,
                op0=ALU.mult, op1=ALU.max, accum_out=run_max[:, n : n + 1],
            )
        neg_max = pool.tile([P, 1], F32, name="neg_max")
        nc.vector.tensor_reduce(neg_max[:], run_max[:], AX.X, ALU.max, negate=True)
        picked = pool.tile([P, I], F32, name="picked")
        nc.vector.tensor_copy(picked[:], scores[:].indirect(offsets[:]))
        px = pool.tile([P, I], F32, name="px")
        z = pool.tile([P, 1], F32, name="z")
        nc.scalar.activation(px[:], picked[:], ACT.Exp, bias=neg_max[:], accum_out=z[:])
        lx = pool.tile([P, I], F32, name="lx")
        nc.vector.tensor_scalar(out=lx[:], in0=picked[:], scalar1=neg_max[:], scalar2=None, op0=ALU.add)
        px_lx = pool.tile([P, I], F32, name="px_lx")
        s = pool.tile([P, 1], F32, name="s")
        nc.vector.scalar_tensor_tensor(
            out=px_lx[:], in0=picked[:], scalar=neg_max[:], in1=px[:], op0=ALU.add, op1=ALU.mult, accum_out=s[:]
        )
        rz = pool.tile([P, 1], F32, name="rz")
        nc.vector.reciprocal(rz[:], z[:])
        dev = pool.tile([P, I], F32, name="dev")
        nc.vector.tensor_scalar(
            out=dev[:], in0=lx[:], scalar1=z[:], scalar2=s[:], op0=ALU.mult, op1=ALU.subtract
        )
        nc.vector.tensor_tensor(spread[:].indirect(offsets[:]), px[:], dev[:], ALU.mult)

        ln_z = pool.tile([P, 1], F32, name="ln_z")
        nc.scalar.activation(ln_z[:], z[:], ACT.Ln)
        mean_aim = pool.tile([P, 1], F32, name="mean_aim")
        nc.scalar.activation(mean_aim[:], s[:], ACT.Identity, bias=aim_col[:], scale=rz[:])
        miss = pool.tile([P, 1], F32, name="miss")
        nc.scalar.activation(miss[:], ln_z[:], ACT.Identity, bias=mean_aim[:], scale=-1.0)
        miss_z = pool.tile([P, 1], F32, name="miss_z")
        nc.scalar.activation(miss_z[:], miss[:], ACT.Copy, scale=rz[:])
        rz512 = pool.tile([P, 1], F32, name="rz512")
        nc.scalar.activation(rz512[:], rz[:], ACT.Copy, scale=512.0)
        factor = pool.tile([P, 1], F32, name="factor")
        nc.scalar.activation(factor[:], miss_z[:], ACT.Copy, scale=rz512[:])

        for n, (lo, hi) in enumerate(runs(OUT_RUNS)):
            result = pool.tile([P, hi - lo], F32, name="result%d" % n)
            nc.vector.scalar_tensor_tensor(
                out=result[:], in0=spread[:, lo:hi], scalar=factor[:], in1=old_sb[:, lo:hi], op0=ALU.mult, op1=ALU.add
            )
            nc.sync.dma_start(out=out[:, lo:hi], in_=result[:])
